import numpy as np
import ml_dtypes


def mxq(x, axis, fmt="e4m3"):
    dtype, down = {"e4m3": (ml_dtypes.float8_e4m3fn, 7), "e5m2": (ml_dtypes.float8_e5m2, 14)}[fmt]
    v = np.moveaxis(np.asarray(x, np.float32).astype(ml_dtypes.bfloat16).astype(np.float64), axis, -1)
    blocks = v.reshape(v.shape[:-1] + (-1, 32))
    amax = np.abs(blocks).max(-1, keepdims=True)
    byte = np.maximum(np.where(amax > 0, np.frexp(amax)[1] - 1 + 127, 0) - down, 1)
    scale = np.exp2(byte - 127.0)
    codes = (blocks / scale).astype(np.float32).astype(dtype).astype(np.float64)
    return np.moveaxis((codes * scale).reshape(v.shape), -1, axis)


WIDE = False


def mx_kscale(k):
    if not WIDE:
        return np.ones(k)
    levels = np.array([10, -10, 5, -5, 0])
    if k % 512:
        return np.exp2(np.random.permutation(np.resize(levels, k // 32))).repeat(32)
    a = np.empty((k // 512, 16))
    for p in range(k // 512):
        a[p, :8] = np.random.permutation(np.resize(levels, 8))
        for g in range(8):
            far = levels[np.abs(levels - a[p, g]) >= 10]
            a[p, g + 8] = far[np.random.randint(len(far))]
    return np.exp2(a.ravel()).repeat(32)


def f64(x):
    return np.asarray(x).astype(np.float64)


def striped(idx):
    return np.tile(idx.reshape(-1, 16).T, (8, 1)).astype(np.uint16)


def unstriped(offs):
    return offs[:16].T.reshape(-1).astype(np.int64)


def pack_weight(w):
    k, n = w.shape
    w = f64(np.asarray(w, np.float32).astype(ml_dtypes.bfloat16)).reshape(k // 32, 32, n)
    amax = np.abs(w).max(1)
    byte = np.clip(np.where(amax > 0, np.frexp(amax)[1] - 1 + 127 - 7, 1), 1, 254)
    scaled = (w * np.exp2(127.0 - byte)[:, None, :]).reshape(k, n).astype(np.float32)
    words = np.ascontiguousarray(scaled.reshape(k // 512, 128, 4, n).transpose(0, 1, 3, 2)).astype(ml_dtypes.float8_e4m3fn).view(np.uint8)
    return words, np.ascontiguousarray(byte.astype(np.uint8).reshape(k // 512, 16, n))


def unpack_weight(words, scales):
    g, p, n, _ = words.shape
    vals = np.ascontiguousarray(words).view(ml_dtypes.float8_e4m3fn).astype(np.float64) * np.repeat(np.exp2(scales.astype(np.float64) - 127.0), 8, axis=1)[..., None]
    return vals.transpose(0, 1, 3, 2).reshape(g * 512, n)


def sigmoid(v):
    return 1.0 / (1.0 + np.exp(-np.maximum(v, -700.0)))


K, T, S, N, U = 512, 2048, 512, 256, 1024
P = 2 ** 7


def setup_inputs():
    n = np.random.standard_normal
    s = mx_kscale(K)[:, None]
    packed_xT = pack_weight(n((K, T)) * s)
    return {
        "x_words": packed_xT[0],
        "x_scales": packed_xT[1],
        "w1": (n((K, N)) / np.sqrt(K) / s).astype(np.float32),
        "w2": (n((K, N)) / np.sqrt(K) / s).astype(np.float32),
        "band": (np.tile(np.random.uniform(0.5, 1.0, S), (P, 1))).astype(np.float32),
        "dist": (n((N, U)) * 0.5).astype(np.float32),
        "wgt": (np.random.uniform(0.2, 3.0, (N, U))).astype(np.float32),
        "wmax": (np.tile(np.random.uniform(1.0, 3.0, S), (P, 1))).astype(np.float32),
        "offs": striped(np.random.permutation(T)[:S]),
        "vox": striped(np.random.permutation(U)[:S]),
    }


def reference(x_words, x_scales, w1, w2, band, dist, wgt, wmax, offs, vox):
    wg = f64(wgt)[:, unstriped(vox)]
    dg = f64(dist)[:, unstriped(vox)]
    xq = unpack_weight(x_words, x_scales)[:, unstriped(offs)]
    yw = mxq(f64(w2), 0, "e4m3").T @ xq
    wn = sigmoid(yw)
    yd = mxq(f64(w1), 0, "e4m3").T @ xq
    td = np.maximum(np.minimum(yd, f64(band)[:1]), -1.0 * f64(band)[:1])
    nd = (wg * dg + wn * td) / (wg + wn)
    return ((nd - td) ** 2) * (np.minimum(wg + wn, f64(wmax)[:1])) + 0.3 * np.abs(dg)

@@ -1,0 +1,181 @@
+from contextlib import ExitStack
+
+import concourse.mybir as mybir
+from concourse.masks import make_identity
+
+F32 = mybir.dt.float32
+BF16 = mybir.dt.bfloat16
+I32 = mybir.dt.int32
+U32 = mybir.dt.uint32
+U16 = mybir.dt.uint16
+U8 = mybir.dt.uint8
+FP8X4 = mybir.dt.float8_e4m3fn_x4
+ALU = mybir.AluOpType
+ACT = mybir.ActivationFunctionType
+
+P = 128
+K, T, S, N, U = 512, 2048, 512, 256, 1024
+PACK = 4
+HALF = S // 2
+FLOPS = 2 * 2 * K * N * S
+ON_SCALAR = []
+
+
+def tile_picked_ytsdf_en_p_kernel(tc, x_words, x_scales, w1, w2, band, dist, wgt, wmax, offs, vox, out):
+    nc = tc.nc
+    with ExitStack() as ctx:
+        sb = ctx.enter_context(tc.tile_pool(name="sb", bufs=1))
+        ps = ctx.enter_context(tc.psum_pool(name="ps", bufs=1))
+
+        offs_t = sb.tile([P, S // 16], U16, name="offs_t")
+        vox_t = sb.tile([P, S // 16], U16, name="vox_t")
+        xw_win = sb.tile([P, T], I32, name="xw_win")
+        xs_win = sb.tile([P, T], U8, name="xs_win")
+        w_raw = [sb.tile([P, PACK, N], F32, name="w_raw%d" % i) for i in range(2)]
+        wgt_win = [sb.tile([P, U], F32, name="wgt_win%d" % b) for b in range(2)]
+        dist_win = [sb.tile([P, U], F32, name="dist_win%d" % b) for b in range(2)]
+        rows = sb.tile([P, P], F32, name="rows")
+        cols = sb.tile([P, 8], F32, name="cols")
+        band2_c = sb.tile([P, 4], F32, name="band2_c")
+        ident = sb.tile([P, P], F32, name="ident")
+
+        nc.vector.memset(xs_win[:].bitcast(I32), 0)
+        nc.gpsimd.memset(rows[:], 0.0)
+        for q in range(4):
+            nc.scalar.dma_start(out=xs_win[32 * q : 32 * q + 4, :].bitcast(I32), in_=x_scales[0, 4 * q : 4 * q + 4, :].bitcast(I32))
+        nc.scalar.dma_start(out=rows[0:4, :], in_=band[0, :].rearrange("(t p) -> t p", p=P))
+        nc.scalar.dma_start(out=rows[4:8, :], in_=wmax[0, :].rearrange("(t p) -> t p", p=P))
+        nc.sync.dma_start(offs_t[:], offs)
+        nc.sync.dma_start(out=w_raw[1][:], in_=w2.rearrange("(p j) n -> p j n", j=PACK))
+        nc.sync.dma_start(out=xw_win[:], in_=x_words[0].rearrange("p n t -> p (n t)").bitcast(I32))
+        nc.sync.dma_start(vox_t[:], vox)
+        nc.sync.dma_start(out=wgt_win[0][:], in_=wgt[0:P, :])
+        nc.sync.dma_start(out=wgt_win[1][:], in_=wgt[P : 2 * P, :])
+        nc.sync.dma_start(out=w_raw[0][:], in_=w1.rearrange("(p j) n -> p j n", j=PACK))
+        nc.sync.dma_start(out=dist_win[0][:], in_=dist[0:P, :])
+        nc.sync.dma_start(out=dist_win[1][:], in_=dist[P : 2 * P, :])
+        make_identity(nc, ident[:])
+
+        def quantise(i):
+            grouped = sb.tile([P, N, PACK], BF16, name="grouped%d" % i, align_bytes=64)
+            codes = sb.tile([P, N], U32, name="codes%d" % i, align_bytes=64)
+            scales = sb.tile([P, N], U8, name="scales%d" % i, align_bytes=64)
+            nc.vector.tensor_copy(
+                out=grouped[:].rearrange("p (c i) t -> p c t i", i=4),
+                in_=w_raw[i][:].rearrange("p t (c i) -> p c t i", i=4),
+            )
+            nc.vector.quantize_mx(out=codes[:].bitcast(FP8X4), scales=scales[:], in_=grouped[:].rearrange("p w j -> p (w j)"))
+            return codes, scales
+
+        def half_list(lst, h):
+            return lst[:, h * (HALF // 16) : (h + 1) * (HALF // 16)]
+
+        def turn(blocks):
+            for n, (dst, src) in enumerate(blocks):
+                nc.tensor.matmul(dst, lhsT=src, rhs=ident[:], is_transpose=True, start=(n == 0), stop=(n == len(blocks) - 1))
+
+        def blocks_of(bank, src):
+            return [(bank[:, a, b * P : (b + 1) * P], src[:, b, a * P : (a + 1) * P]) for b in range(2) for a in range(2)]
+
+        w2c, w2s = quantise(1)
+        xs = sb.tile([P, S], U8, name="xs", align_bytes=64)
+        nc.vector.tensor_copy(xs[:], xs_win[:].indirect(offs_t[:]))
+        cols_ps = ps.tile([P, P], F32, name="cols_ps", tag="bankC0")
+        turn([(cols_ps[:], rows[:])])
+        nc.vector.tensor_copy(cols[:], cols_ps[:, 0:8])
+        nc.vector.tensor_scalar(band2_c[:], cols_ps[:, 0:4], 2.0, 0.0, ALU.mult, ALU.add)
+        xw, wn = [], []
+        for h in range(2):
+            xw.append(sb.tile([P, HALF], U32, name="xw%d" % h, align_bytes=64))
+            nc.vector.tensor_copy(xw[h][:], xw_win[:].bitcast(U32).indirect(half_list(offs_t, h)))
+            yw = ps.tile([P, 2, HALF], F32, name="yw%d" % h, tag="bankA%d" % h)
+            for b in range(2):
+                nc.tensor.matmul_mx(
+                    out=yw[:, b, :],
+                    lhsT=w2c[:, b * P : (b + 1) * P].bitcast(FP8X4),
+                    lhsT_scale=w2s[:, b * P : (b + 1) * P],
+                    rhs=xw[h][:].bitcast(FP8X4),
+                    rhs_scale=xs[:, h * HALF : (h + 1) * HALF],
+                    start=True,
+                    stop=True,
+                )
+            wn.append(sb.tile([P, 2, HALF], F32, name="wn%d" % h))
+            nc.scalar.activation(wn[h][:], yw[:], ACT.Sigmoid)
+
+        def gather(win, name):
+            got = [sb.tile([P, 2, HALF], F32, name="%s%d" % (name, h)) for h in range(2)]
+            for b in range(2):
+                for h in range(2):
+                    picked = win[b][:].indirect(half_list(vox_t, h))
+                    if [name, b, h] in ON_SCALAR:
+                        nc.scalar.activation(got[h][:, b, :], picked, ACT.Copy)
+                    else:
+                        nc.vector.tensor_copy(got[h][:, b, :], picked)
+            return got
+
+        wg = gather(wgt_win, "wg")
+        sT, wgT, r = [], [], []
+        for h in range(2):
+            sT.append(ps.tile([P, 2, N], F32, name="sT%d" % h, tag="bankA%d" % h))
+            turn(blocks_of(sT[h], wn[h]) + blocks_of(sT[h], wg[h]))
+        for h in range(2):
+            z = sb.tile([P, 2, N], F32, name="z%d" % h)
+            r.append(sb.tile([P, 2, N], F32, name="r%d" % h))
+            nc.scalar.activation(z[:], sT[h][:], ACT.Abs_reciprocal_sqrt)
+            nc.scalar.activation(r[h][:], z[:], ACT.Square)
+        for h in range(2):
+            wgT.append(ps.tile([P, 2, N], F32, name="wgT%d" % h, tag="bankC%d" % h))
+            turn(blocks_of(wgT[h], wg[h]))
+
+        w1c, w1s = quantise(0)
+        v = []
+        for h in range(2):
+            yd = ps.tile([P, 2, N], F32, name="yd%d" % h, tag="bankB%d" % h)
+            v.append(sb.tile([P, 2, N], F32, name="v%d" % h))
+            for a in range(2):
+                jt = 2 * h + a
+                nc.tensor.matmul_mx(
+                    out=yd[:, a, :],
+                    lhsT=xw[h][:, a * P : (a + 1) * P].bitcast(FP8X4),
+                    lhsT_scale=xs[:, jt * P : (jt + 1) * P],
+                    rhs=w1c[:].bitcast(FP8X4),
+                    rhs_scale=w1s[:],
+                    start=True,
+                    stop=True,
+                )
+            for a in range(2):
+                jt = 2 * h + a
+                nc.scalar.activation(v[h][:, a, :], yd[:, a, :], ACT.Relu, bias=cols[:, jt : jt + 1], scale=-1.0)
+
+        dg = gather(dist_win, "dg")
+        dgT, t = [], []
+        for h in range(2):
+            dgT.append(ps.tile([P, 2, N], F32, name="dgT%d" % h))
+            turn(blocks_of(dgT[h], dg[h]))
+        for h in range(2):
+            t.append(sb.tile([P, 2, N], F32, name="t%d" % h))
+            nc.vector.tensor_tensor(t[h][:], wgT[h][:], r[h][:], ALU.mult)
+        x, q, q2, e, ab = [], [], [], [], []
+        for h in range(2):
+            x.append(sb.tile([P, 2, N], F32, name="x%d" % h))
+            q.append(sb.tile([P, 2, N], F32, name="q%d" % h))
+            q2.append(sb.tile([P, 2, N], F32, name="q2%d" % h))
+            ab.append(sb.tile([P, 2, N], F32, name="ab%d" % h))
+            for a in range(2):
+                jt = 2 * h + a
+                nc.vector.scalar_tensor_tensor(x[h][:, a, :], v[h][:, a, :], band2_c[:, jt : jt + 1], dgT[h][:, a, :], ALU.min, ALU.add)
+            for a in range(2):
+                jt = 2 * h + a
+                nc.vector.scalar_tensor_tensor(q[h][:, a, :], x[h][:, a, :], cols[:, jt : jt + 1], t[h][:, a, :], ALU.subtract, ALU.mult)
+            nc.scalar.activation(ab[h][:], dgT[h][:], ACT.Abs, scale=0.3)
+            for a in range(2):
+                nc.scalar.activation(q2[h][:, a, :], q[h][:, a, :], ACT.Square)
+        for jt in range(4):
+            h, a = divmod(jt, 2)
+            e = sb.tile([P, N], F32, name="e%d" % jt)
+            nc.vector.scalar_tensor_tensor(e[:], sT[h][:, a, :], cols[:, 4 + jt : 5 + jt], q2[h][:, a, :], ALU.min, ALU.mult)
+            res_ps = ps.tile([P, 2, P], F32, name="res_ps%d" % jt, tag="bank%s%d" % ("BC"[h], a))
+            turn([(res_ps[:, b, :], src[:, b * P : (b + 1) * P]) for src in (ab[h][:, a, :], e[:]) for b in range(2)])
+            res = sb.tile([P, 2, P], F32, name="res%d" % jt)
+            nc.scalar.copy(res[:], res_ps[:])
+            nc.sync.dma_start(out=out[:, jt * P : (jt + 1) * P].rearrange("(b p) j -> p b j", p=P), in_=res[:])

@@ -18,7 +18,8 @@ K, T, S, N, U = 512, 2048, 512, 256, 1024
 PACK = 4
 HALF = S // 2
 FLOPS = 2 * 2 * K * N * S
-ON_SCALAR = []
+EVAC_S = [0,1]
+S_GATHER = [[0,1]]
 
 
 def tile_picked_ytsdf_en_p_kernel(tc, x_words, x_scales, w1, w2, band, dist, wgt, wmax, offs, vox, out):
@@ -31,38 +32,37 @@ def tile_picked_ytsdf_en_p_kernel(tc, x_words, x_scales, w1, w2, band, dist, wgt
         vox_t = sb.tile([P, S // 16], U16, name="vox_t")
         xw_win = sb.tile([P, T], I32, name="xw_win")
         xs_win = sb.tile([P, T], U8, name="xs_win")
-        w_raw = [sb.tile([P, PACK, N], F32, name="w_raw%d" % i) for i in range(2)]
+        w2_raw = sb.tile([P, PACK, N], F32, name="w2_raw")
+        w1_raw = sb.tile([P, PACK, N], F32, name="w1_raw")
         wgt_win = [sb.tile([P, U], F32, name="wgt_win%d" % b) for b in range(2)]
-        dist_win = [sb.tile([P, U], F32, name="dist_win%d" % b) for b in range(2)]
+        dist_win = [sb.tile([P, U], F32, name="dist_win%d" % b, tag="dist_win%d" % b) for b in range(2)]
         rows = sb.tile([P, P], F32, name="rows")
-        cols = sb.tile([P, 8], F32, name="cols")
-        band2_c = sb.tile([P, 4], F32, name="band2_c")
         ident = sb.tile([P, P], F32, name="ident")
 
-        nc.vector.memset(xs_win[:].bitcast(I32), 0)
+        nc.gpsimd.memset(xs_win[:].bitcast(I32), 0)
         nc.gpsimd.memset(rows[:], 0.0)
-        for q in range(4):
-            nc.scalar.dma_start(out=xs_win[32 * q : 32 * q + 4, :].bitcast(I32), in_=x_scales[0, 4 * q : 4 * q + 4, :].bitcast(I32))
-        nc.scalar.dma_start(out=rows[0:4, :], in_=band[0, :].rearrange("(t p) -> t p", p=P))
-        nc.scalar.dma_start(out=rows[4:8, :], in_=wmax[0, :].rearrange("(t p) -> t p", p=P))
         nc.sync.dma_start(offs_t[:], offs)
-        nc.sync.dma_start(out=w_raw[1][:], in_=w2.rearrange("(p j) n -> p j n", j=PACK))
+        nc.sync.dma_start(out=w2_raw[:], in_=w2.rearrange("(p j) n -> p j n", j=PACK))
+        for q in range(4):
+            nc.sync.dma_start(out=xs_win[32 * q : 32 * q + 4, :].bitcast(I32), in_=x_scales[0, 4 * q : 4 * q + 4, :].bitcast(I32))
         nc.sync.dma_start(out=xw_win[:], in_=x_words[0].rearrange("p n t -> p (n t)").bitcast(I32))
         nc.sync.dma_start(vox_t[:], vox)
-        nc.sync.dma_start(out=wgt_win[0][:], in_=wgt[0:P, :])
-        nc.sync.dma_start(out=wgt_win[1][:], in_=wgt[P : 2 * P, :])
-        nc.sync.dma_start(out=w_raw[0][:], in_=w1.rearrange("(p j) n -> p j n", j=PACK))
-        nc.sync.dma_start(out=dist_win[0][:], in_=dist[0:P, :])
-        nc.sync.dma_start(out=dist_win[1][:], in_=dist[P : 2 * P, :])
+        nc.sync.dma_start(out=rows[0:4, :], in_=band[0, :].rearrange("(t p) -> t p", p=P))
+        nc.sync.dma_start(out=rows[4:8, :], in_=wmax[0, :].rearrange("(t p) -> t p", p=P))
+        for b in range(2):
+            nc.sync.dma_start(out=wgt_win[b][:], in_=wgt[b * P : (b + 1) * P, :])
+        nc.sync.dma_start(out=w1_raw[:], in_=w1.rearrange("(p j) n -> p j n", j=PACK))
+        for b in range(2):
+            nc.sync.dma_start(out=dist_win[b][:], in_=dist[b * P : (b + 1) * P, :])
         make_identity(nc, ident[:])
 
-        def quantise(i):
-            grouped = sb.tile([P, N, PACK], BF16, name="grouped%d" % i, align_bytes=64)
-            codes = sb.tile([P, N], U32, name="codes%d" % i, align_bytes=64)
-            scales = sb.tile([P, N], U8, name="scales%d" % i, align_bytes=64)
+        def quantise(name, raw):
+            grouped = sb.tile([P, N, PACK], BF16, name=name + "_grouped", align_bytes=64)
+            codes = sb.tile([P, N], U32, name=name + "_codes", align_bytes=64)
+            scales = sb.tile([P, N], U8, name=name + "_scales", align_bytes=64)
             nc.vector.tensor_copy(
                 out=grouped[:].rearrange("p (c i) t -> p c t i", i=4),
-                in_=w_raw[i][:].rearrange("p t (c i) -> p c t i", i=4),
+                in_=raw.rearrange("p t (c i) -> p c t i", i=4),
             )
             nc.vector.quantize_mx(out=codes[:].bitcast(FP8X4), scales=scales[:], in_=grouped[:].rearrange("p w j -> p (w j)"))
             return codes, scales
@@ -77,16 +77,12 @@ def tile_picked_ytsdf_en_p_kernel(tc, x_words, x_scales, w1, w2, band, dist, wgt
         def blocks_of(bank, src):
             return [(bank[:, a, b * P : (b + 1) * P], src[:, b, a * P : (a + 1) * P]) for b in range(2) for a in range(2)]
 
-        w2c, w2s = quantise(1)
+        w2c, w2s = quantise("w2", w2_raw[:])
         xs = sb.tile([P, S], U8, name="xs", align_bytes=64)
         nc.vector.tensor_copy(xs[:], xs_win[:].indirect(offs_t[:]))
-        cols_ps = ps.tile([P, P], F32, name="cols_ps", tag="bankC0")
-        turn([(cols_ps[:], rows[:])])
-        nc.vector.tensor_copy(cols[:], cols_ps[:, 0:8])
-        nc.vector.tensor_scalar(band2_c[:], cols_ps[:, 0:4], 2.0, 0.0, ALU.mult, ALU.add)
-        xw, wn = [], []
+        xw = [sb.tile([P, HALF], U32, name="xw%d" % h, align_bytes=64) for h in range(2)]
+        wn = []
         for h in range(2):
-            xw.append(sb.tile([P, HALF], U32, name="xw%d" % h, align_bytes=64))
             nc.vector.tensor_copy(xw[h][:], xw_win[:].bitcast(U32).indirect(half_list(offs_t, h)))
             yw = ps.tile([P, 2, HALF], F32, name="yw%d" % h, tag="bankA%d" % h)
             for b in range(2):
@@ -102,40 +98,28 @@ def tile_picked_ytsdf_en_p_kernel(tc, x_words, x_scales, w1, w2, band, dist, wgt
             wn.append(sb.tile([P, 2, HALF], F32, name="wn%d" % h))
             nc.scalar.activation(wn[h][:], yw[:], ACT.Sigmoid)
 
-        def gather(win, name):
-            got = [sb.tile([P, 2, HALF], F32, name="%s%d" % (name, h)) for h in range(2)]
-            for b in range(2):
-                for h in range(2):
-                    picked = win[b][:].indirect(half_list(vox_t, h))
-                    if [name, b, h] in ON_SCALAR:
-                        nc.scalar.activation(got[h][:, b, :], picked, ACT.Copy)
-                    else:
-                        nc.vector.tensor_copy(got[h][:, b, :], picked)
-            return got
-
-        wg = gather(wgt_win, "wg")
-        sT, wgT, r = [], [], []
+        cols_ps = ps.tile([P, P], F32, name="cols_ps", tag="bankC0")
+        turn([(cols_ps[:], rows[:])])
+        cols = sb.tile([P, 12], F32, name="cols")
+        nc.scalar.activation(cols[:, 0:8], cols_ps[:, 0:8], ACT.Copy)
+        nc.scalar.activation(cols[:, 8:12], cols_ps[:, 0:4], ACT.Copy, scale=2.0)
+        wg = [sb.tile([P, 2, HALF], F32, name="wg%d" % h) for h in range(2)]
+        for b in range(2):
+            for h in range(2):
+                nc.vector.tensor_copy(wg[h][:, b, :], wgt_win[b][:].indirect(half_list(vox_t, h)))
+        sT = []
         for h in range(2):
             sT.append(ps.tile([P, 2, N], F32, name="sT%d" % h, tag="bankA%d" % h))
             turn(blocks_of(sT[h], wn[h]) + blocks_of(sT[h], wg[h]))
-        for h in range(2):
-            z = sb.tile([P, 2, N], F32, name="z%d" % h)
-            r.append(sb.tile([P, 2, N], F32, name="r%d" % h))
-            nc.scalar.activation(z[:], sT[h][:], ACT.Abs_reciprocal_sqrt)
-            nc.scalar.activation(r[h][:], z[:], ACT.Square)
-        for h in range(2):
-            wgT.append(ps.tile([P, 2, N], F32, name="wgT%d" % h, tag="bankC%d" % h))
-            turn(blocks_of(wgT[h], wg[h]))
 
-        w1c, w1s = quantise(0)
-        v = []
+        w1c, w1s = quantise("w1", w1_raw[:])
+        yd = []
         for h in range(2):
-            yd = ps.tile([P, 2, N], F32, name="yd%d" % h, tag="bankB%d" % h)
-            v.append(sb.tile([P, 2, N], F32, name="v%d" % h))
+            yd.append(ps.tile([P, 2, N], F32, name="yd%d" % h, tag="bankB%d" % h))
             for a in range(2):
                 jt = 2 * h + a
                 nc.tensor.matmul_mx(
-                    out=yd[:, a, :],
+                    out=yd[h][:, a, :],
                     lhsT=xw[h][:, a * P : (a + 1) * P].bitcast(FP8X4),
                     lhsT_scale=xs[:, jt * P : (jt + 1) * P],
                     rhs=w1c[:].bitcast(FP8X4),
@@ -143,39 +127,68 @@ def tile_picked_ytsdf_en_p_kernel(tc, x_words, x_scales, w1, w2, band, dist, wgt
                     start=True,
                     stop=True,
                 )
+        wgT = []
+        for h in range(2):
+            wgT.append(ps.tile([P, 2, N], F32, name="wgT%d" % h, tag="bankC%d" % h))
+            turn(blocks_of(wgT[h], wg[h]))
+
+        z = [sb.tile([P, 2, N], F32, name="z%d" % h) for h in range(2)]
+        r = [sb.tile([P, 2, N], F32, name="r%d" % h) for h in range(2)]
+        v = [sb.tile([P, 2, N], F32, name="v%d" % h) for h in range(2)]
+        dg = [sb.tile([P, 2, HALF], F32, name="dg%d" % h) for h in range(2)]
+        for h in range(2):
+            nc.scalar.activation(z[h][:], sT[h][:], ACT.Abs_reciprocal_sqrt)
+        for b in range(2):
+            for h in range(2):
+                if [b, h] not in S_GATHER:
+                    nc.vector.tensor_copy(dg[h][:, b, :], dist_win[b][:].indirect(half_list(vox_t, h)))
+        dgT = []
+
+        def below_band(h):
             for a in range(2):
                 jt = 2 * h + a
-                nc.scalar.activation(v[h][:, a, :], yd[:, a, :], ACT.Relu, bias=cols[:, jt : jt + 1], scale=-1.0)
+                nc.scalar.activation(v[h][:, a, :], yd[h][:, a, :], ACT.Relu, bias=cols[:, jt : jt + 1], scale=-1.0)
 
-        dg = gather(dist_win, "dg")
-        dgT, t = [], []
+        nc.scalar.activation(r[0][:], z[0][:], ACT.Square)
+        below_band(0)
+        nc.scalar.activation(r[1][:], z[1][:], ACT.Square)
+        for b, h in S_GATHER:
+            nc.scalar.activation(dg[h][:, b, :], dist_win[b][:].indirect(half_list(vox_t, h)), ACT.Copy)
+        below_band(1)
         for h in range(2):
             dgT.append(ps.tile([P, 2, N], F32, name="dgT%d" % h))
             turn(blocks_of(dgT[h], dg[h]))
+        x, q, q2, ab, res_ps = [], [], [], [], []
         for h in range(2):
-            t.append(sb.tile([P, 2, N], F32, name="t%d" % h))
-            nc.vector.tensor_tensor(t[h][:], wgT[h][:], r[h][:], ALU.mult)
-        x, q, q2, e, ab = [], [], [], [], []
-        for h in range(2):
+            t = sb.tile([P, 2, N], F32, name="t%d" % h, tag=("dist_win1", "t1")[h])
             x.append(sb.tile([P, 2, N], F32, name="x%d" % h))
             q.append(sb.tile([P, 2, N], F32, name="q%d" % h))
             q2.append(sb.tile([P, 2, N], F32, name="q2%d" % h))
-            ab.append(sb.tile([P, 2, N], F32, name="ab%d" % h))
+            nc.vector.tensor_tensor(t[:], wgT[h][:], r[h][:], ALU.mult)
             for a in range(2):
                 jt = 2 * h + a
-                nc.vector.scalar_tensor_tensor(x[h][:, a, :], v[h][:, a, :], band2_c[:, jt : jt + 1], dgT[h][:, a, :], ALU.min, ALU.add)
+                nc.vector.scalar_tensor_tensor(x[h][:, a, :], v[h][:, a, :], cols[:, 8 + jt : 9 + jt], dgT[h][:, a, :], ALU.min, ALU.add)
             for a in range(2):
                 jt = 2 * h + a
-                nc.vector.scalar_tensor_tensor(q[h][:, a, :], x[h][:, a, :], cols[:, jt : jt + 1], t[h][:, a, :], ALU.subtract, ALU.mult)
-            nc.scalar.activation(ab[h][:], dgT[h][:], ACT.Abs, scale=0.3)
+                nc.vector.scalar_tensor_tensor(q[h][:, a, :], x[h][:, a, :], cols[:, jt : jt + 1], t[:, a, :], ALU.subtract, ALU.mult)
             for a in range(2):
                 nc.scalar.activation(q2[h][:, a, :], q[h][:, a, :], ACT.Square)
+        for h in range(2):
+            ab.append(sb.tile([P, 2, HALF], F32, name="ab%d" % h))
+            src = dgT[h] if 2 * h in EVAC_S else dg[h]
+            nc.scalar.activation(ab[h][:], src[:], ACT.Abs, scale=0.3)
         for jt in range(4):
             h, a = divmod(jt, 2)
             e = sb.tile([P, N], F32, name="e%d" % jt)
             nc.vector.scalar_tensor_tensor(e[:], sT[h][:, a, :], cols[:, 4 + jt : 5 + jt], q2[h][:, a, :], ALU.min, ALU.mult)
-            res_ps = ps.tile([P, 2, P], F32, name="res_ps%d" % jt, tag="bank%s%d" % ("BC"[h], a))
-            turn([(res_ps[:, b, :], src[:, b * P : (b + 1) * P]) for src in (ab[h][:, a, :], e[:]) for b in range(2)])
+            res_ps.append(ps.tile([P, 2, P], F32, name="res_ps%d" % jt, tag="bank%s%d" % ("BC"[h], a)))
+            srcs = (ab[h][:, a, :], e[:]) if jt in EVAC_S else (e[:],)
+            turn([(res_ps[jt][:, b, :], src[:, b * P : (b + 1) * P]) for src in srcs for b in range(2)])
+        for jt in range(4):
+            h, a = divmod(jt, 2)
             res = sb.tile([P, 2, P], F32, name="res%d" % jt)
-            nc.scalar.copy(res[:], res_ps[:])
+            if jt in EVAC_S:
+                nc.scalar.copy(res[:], res_ps[jt][:])
+            else:
+                nc.vector.tensor_tensor(res[:], res_ps[jt][:], ab[h][:, :, a * P : (a + 1) * P], ALU.add)
             nc.sync.dma_start(out=out[:, jt * P : (jt + 1) * P].rearrange("(b p) j -> p b j", p=P), in_=res[:])

from contextlib import ExitStack

import concourse.mybir as mybir
from concourse.masks import make_identity

F32 = mybir.dt.float32
BF16 = mybir.dt.bfloat16
I32 = mybir.dt.int32
U32 = mybir.dt.uint32
U16 = mybir.dt.uint16
U8 = mybir.dt.uint8
FP8X4 = mybir.dt.float8_e4m3fn_x4
ALU = mybir.AluOpType
ACT = mybir.ActivationFunctionType

P = 128
K, T, S, N, U = 512, 2048, 512, 256, 1024
PACK = 4
HALF = S // 2
FLOPS = 2 * 2 * K * N * S
EVAC_S = [0,1]
S_GATHER = [[0,1]]


def tile_picked_ytsdf_en_p_kernel(tc, x_words, x_scales, w1, w2, band, dist, wgt, wmax, offs, vox, out):
    nc = tc.nc
    with ExitStack() as ctx:
        sb = ctx.enter_context(tc.tile_pool(name="sb", bufs=1))
        ps = ctx.enter_context(tc.psum_pool(name="ps", bufs=1))

        offs_t = sb.tile([P, S // 16], U16, name="offs_t")
        vox_t = sb.tile([P, S // 16], U16, name="vox_t")
        xw_win = sb.tile([P, T], I32, name="xw_win")
        xs_win = sb.tile([P, T], U8, name="xs_win")
        w2_raw = sb.tile([P, PACK, N], F32, name="w2_raw")
        w1_raw = sb.tile([P, PACK, N], F32, name="w1_raw")
        wgt_win = [sb.tile([P, U], F32, name="wgt_win%d" % b) for b in range(2)]
        dist_win = [sb.tile([P, U], F32, name="dist_win%d" % b, tag="dist_win%d" % b) for b in range(2)]
        rows = sb.tile([P, P], F32, name="rows")
        ident = sb.tile([P, P], F32, name="ident")

        nc.gpsimd.memset(xs_win[:].bitcast(I32), 0)
        nc.gpsimd.memset(rows[:], 0.0)
        nc.sync.dma_start(offs_t[:], offs)
        nc.sync.dma_start(out=w2_raw[:], in_=w2.rearrange("(p j) n -> p j n", j=PACK))
        for q in range(4):
            nc.sync.dma_start(out=xs_win[32 * q : 32 * q + 4, :].bitcast(I32), in_=x_scales[0, 4 * q : 4 * q + 4, :].bitcast(I32))
        nc.sync.dma_start(out=xw_win[:], in_=x_words[0].rearrange("p n t -> p (n t)").bitcast(I32))
        nc.sync.dma_start(vox_t[:], vox)
        nc.sync.dma_start(out=rows[0:4, :], in_=band[0, :].rearrange("(t p) -> t p", p=P))
        nc.sync.dma_start(out=rows[4:8, :], in_=wmax[0, :].rearrange("(t p) -> t p", p=P))
        for b in range(2):
            nc.sync.dma_start(out=wgt_win[b][:], in_=wgt[b * P : (b + 1) * P, :])
        nc.sync.dma_start(out=w1_raw[:], in_=w1.rearrange("(p j) n -> p j n", j=PACK))
        for b in range(2):
            nc.sync.dma_start(out=dist_win[b][:], in_=dist[b * P : (b + 1) * P, :])
        make_identity(nc, ident[:])

        def quantise(name, raw):
            grouped = sb.tile([P, N, PACK], BF16, name=name + "_grouped", align_bytes=64)
            codes = sb.tile([P, N], U32, name=name + "_codes", align_bytes=64)
            scales = sb.tile([P, N], U8, name=name + "_scales", align_bytes=64)
            nc.vector.tensor_copy(
                out=grouped[:].rearrange("p (c i) t -> p c t i", i=4),
                in_=raw.rearrange("p t (c i) -> p c t i", i=4),
            )
            nc.vector.quantize_mx(out=codes[:].bitcast(FP8X4), scales=scales[:], in_=grouped[:].rearrange("p w j -> p (w j)"))
            return codes, scales

        def half_list(lst, h):
            return lst[:, h * (HALF // 16) : (h + 1) * (HALF // 16)]

        def turn(blocks):
            for n, (dst, src) in enumerate(blocks):
                nc.tensor.matmul(dst, lhsT=src, rhs=ident[:], is_transpose=True, start=(n == 0), stop=(n == len(blocks) - 1))

        def blocks_of(bank, src):
            return [(bank[:, a, b * P : (b + 1) * P], src[:, b, a * P : (a + 1) * P]) for b in range(2) for a in range(2)]

        w2c, w2s = quantise("w2", w2_raw[:])
        xs = sb.tile([P, S], U8, name="xs", align_bytes=64)
        nc.vector.tensor_copy(xs[:], xs_win[:].indirect(offs_t[:]))
        xw = [sb.tile([P, HALF], U32, name="xw%d" % h, align_bytes=64) for h in range(2)]
        wn = []
        for h in range(2):
            nc.vector.tensor_copy(xw[h][:], xw_win[:].bitcast(U32).indirect(half_list(offs_t, h)))
            yw = ps.tile([P, 2, HALF], F32, name="yw%d" % h, tag="bankA%d" % h)
            for b in range(2):
                nc.tensor.matmul_mx(
                    out=yw[:, b, :],
                    lhsT=w2c[:, b * P : (b + 1) * P].bitcast(FP8X4),
                    lhsT_scale=w2s[:, b * P : (b + 1) * P],
                    rhs=xw[h][:].bitcast(FP8X4),
                    rhs_scale=xs[:, h * HALF : (h + 1) * HALF],
                    start=True,
                    stop=True,
                )
            wn.append(sb.tile([P, 2, HALF], F32, name="wn%d" % h))
            nc.scalar.activation(wn[h][:], yw[:], ACT.Sigmoid)

        cols_ps = ps.tile([P, P], F32, name="cols_ps", tag="bankC0")
        turn([(cols_ps[:], rows[:])])
        cols = sb.tile([P, 12], F32, name="cols")
        nc.scalar.activation(cols[:, 0:8], cols_ps[:, 0:8], ACT.Copy)
        nc.scalar.activation(cols[:, 8:12], cols_ps[:, 0:4], ACT.Copy, scale=2.0)
        wg = [sb.tile([P, 2, HALF], F32, name="wg%d" % h) for h in range(2)]
        for b in range(2):
            for h in range(2):
                nc.vector.tensor_copy(wg[h][:, b, :], wgt_win[b][:].indirect(half_list(vox_t, h)))
        sT = []
        for h in range(2):
            sT.append(ps.tile([P, 2, N], F32, name="sT%d" % h, tag="bankA%d" % h))
            turn(blocks_of(sT[h], wn[h]) + blocks_of(sT[h], wg[h]))

        w1c, w1s = quantise("w1", w1_raw[:])
        yd = []
        for h in range(2):
            yd.append(ps.tile([P, 2, N], F32, name="yd%d" % h, tag="bankB%d" % h))
            for a in range(2):
                jt = 2 * h + a
                nc.tensor.matmul_mx(
                    out=yd[h][:, a, :],
                    lhsT=xw[h][:, a * P : (a + 1) * P].bitcast(FP8X4),
                    lhsT_scale=xs[:, jt * P : (jt + 1) * P],
                    rhs=w1c[:].bitcast(FP8X4),
                    rhs_scale=w1s[:],
                    start=True,
                    stop=True,
                )
        wgT = []
        for h in range(2):
            wgT.append(ps.tile([P, 2, N], F32, name="wgT%d" % h, tag="bankC%d" % h))
            turn(blocks_of(wgT[h], wg[h]))

        z = [sb.tile([P, 2, N], F32, name="z%d" % h) for h in range(2)]
        r = [sb.tile([P, 2, N], F32, name="r%d" % h) for h in range(2)]
        v = [sb.tile([P, 2, N], F32, name="v%d" % h) for h in range(2)]
        dg = [sb.tile([P, 2, HALF], F32, name="dg%d" % h) for h in range(2)]
        for h in range(2):
            nc.scalar.activation(z[h][:], sT[h][:], ACT.Abs_reciprocal_sqrt)
        for b in range(2):
            for h in range(2):
                if [b, h] not in S_GATHER:
                    nc.vector.tensor_copy(dg[h][:, b, :], dist_win[b][:].indirect(half_list(vox_t, h)))
        dgT = []

        def below_band(h):
            for a in range(2):
                jt = 2 * h + a
                nc.scalar.activation(v[h][:, a, :], yd[h][:, a, :], ACT.Relu, bias=cols[:, jt : jt + 1], scale=-1.0)

        nc.scalar.activation(r[0][:], z[0][:], ACT.Square)
        below_band(0)
        nc.scalar.activation(r[1][:], z[1][:], ACT.Square)
        for b, h in S_GATHER:
            nc.scalar.activation(dg[h][:, b, :], dist_win[b][:].indirect(half_list(vox_t, h)), ACT.Copy)
        below_band(1)
        for h in range(2):
            dgT.append(ps.tile([P, 2, N], F32, name="dgT%d" % h))
            turn(blocks_of(dgT[h], dg[h]))
        x, q, q2, ab, res_ps = [], [], [], [], []
        for h in range(2):
            t = sb.tile([P, 2, N], F32, name="t%d" % h, tag=("dist_win1", "t1")[h])
            x.append(sb.tile([P, 2, N], F32, name="x%d" % h))
            q.append(sb.tile([P, 2, N], F32, name="q%d" % h))
            q2.append(sb.tile([P, 2, N], F32, name="q2%d" % h))
            nc.vector.tensor_tensor(t[:], wgT[h][:], r[h][:], ALU.mult)
            for a in range(2):
                jt = 2 * h + a
                nc.vector.scalar_tensor_tensor(x[h][:, a, :], v[h][:, a, :], cols[:, 8 + jt : 9 + jt], dgT[h][:, a, :], ALU.min, ALU.add)
            for a in range(2):
                jt = 2 * h + a
                nc.vector.scalar_tensor_tensor(q[h][:, a, :], x[h][:, a, :], cols[:, jt : jt + 1], t[:, a, :], ALU.subtract, ALU.mult)
            for a in range(2):
                nc.scalar.activation(q2[h][:, a, :], q[h][:, a, :], ACT.Square)
        for h in range(2):
            ab.append(sb.tile([P, 2, HALF], F32, name="ab%d" % h))
            src = dgT[h] if 2 * h in EVAC_S else dg[h]
            nc.scalar.activation(ab[h][:], src[:], ACT.Abs, scale=0.3)
        for jt in range(4):
            h, a = divmod(jt, 2)
            e = sb.tile([P, N], F32, name="e%d" % jt)
            nc.vector.scalar_tensor_tensor(e[:], sT[h][:, a, :], cols[:, 4 + jt : 5 + jt], q2[h][:, a, :], ALU.min, ALU.mult)
            res_ps.append(ps.tile([P, 2, P], F32, name="res_ps%d" % jt, tag="bank%s%d" % ("BC"[h], a)))
            srcs = (ab[h][:, a, :], e[:]) if jt in EVAC_S else (e[:],)
            turn([(res_ps[jt][:, b, :], src[:, b * P : (b + 1) * P]) for src in srcs for b in range(2)])
        for jt in range(4):
            h, a = divmod(jt, 2)
            res = sb.tile([P, 2, P], F32, name="res%d" % jt)
            if jt in EVAC_S:
                nc.scalar.copy(res[:], res_ps[jt][:])
            else:
                nc.vector.tensor_tensor(res[:], res_ps[jt][:], ab[h][:, :, a * P : (a + 1) * P], ALU.add)
            nc.sync.dma_start(out=out[:, jt * P : (jt + 1) * P].rearrange("(b p) j -> p b j", p=P), in_=res[:])
